import numpy as np
import ml_dtypes


def mxq(x, axis, fmt="e4m3"):
    dtype, down = {"e4m3": (ml_dtypes.float8_e4m3fn, 7), "e5m2": (ml_dtypes.float8_e5m2, 14)}[fmt]
    v = np.moveaxis(np.asarray(x, np.float32).astype(ml_dtypes.bfloat16).astype(np.float64), axis, -1)
    blocks = v.reshape(v.shape[:-1] + (-1, 32))
    amax = np.abs(blocks).max(-1, keepdims=True)
    byte = np.maximum(np.where(amax > 0, np.frexp(amax)[1] - 1 + 127, 0) - down, 1)
    scale = np.exp2(byte - 127.0)
    codes = (blocks / scale).astype(np.float32).astype(dtype).astype(np.float64)
    return np.moveaxis((codes * scale).reshape(v.shape), -1, axis)


WIDE = False


def mx_kscale(k):
    if not WIDE:
        return np.ones(k)
    levels = np.array([10, -10, 5, -5, 0])
    if k % 512:
        return np.exp2(np.random.permutation(np.resize(levels, k // 32))).repeat(32)
    a = np.empty((k // 512, 16))
    for p in range(k // 512):
        a[p, :8] = np.random.permutation(np.resize(levels, 8))
        for g in range(8):
            far = levels[np.abs(levels - a[p, g]) >= 10]
            a[p, g + 8] = far[np.random.randint(len(far))]
    return np.exp2(a.ravel()).repeat(32)


def f64(x):
    return np.asarray(x).astype(np.float64)


def striped(idx):
    return np.tile(idx.reshape(-1, 16).T, (8, 1)).astype(np.uint16)


def unstriped(offs):
    return offs[:16].T.reshape(-1).astype(np.int64)


K, T, S, N = 1536, 2048, 1024, 128


def setup_inputs():
    n = np.random.standard_normal
    s = mx_kscale(K)[:, None]
    return {
        "xT": (n((K, S)) * s).astype(np.float32),
        "w": (n((K, N)) / np.sqrt(K) / s).astype(np.float32),
        "gate": np.tile(np.random.uniform(0.2, 1.0, S), (N, 1)).astype(np.float32),
        "offs": striped(np.random.permutation(T)[:S]),
    }


def reference(xT, w, gate, offs):
    idx = unstriped(offs)
    xq = mxq(f64(xT), 0, "e4m3")
    y = mxq(f64(w), 0, "e4m3").T @ xq
    out = np.zeros((N, T))
    out[:, idx] = f64(gate) * y
    return out

@@ -1,0 +1,130 @@
+from contextlib import ExitStack
+
+import concourse.mybir as mybir
+
+K, S, N, T = 1536, 1024, 128, 2048
+FLOPS = 2 * K * S * N
+
+F32 = mybir.dt.float32
+BF16 = mybir.dt.bfloat16
+U32 = mybir.dt.uint32
+U16 = mybir.dt.uint16
+U8 = mybir.dt.uint8
+FP8X4 = mybir.dt.float8_e4m3fn_x4
+
+P = 128
+PACK = 4
+K_PASS = P * PACK
+PASSES = K // K_PASS
+HALF = 512
+PIECE = 256
+
+
+def interleave(copy, grouped, raw, lo, hi):
+    copy(
+        out=grouped[:, lo:hi, :].rearrange("p (c i) j -> p c j i", i=4),
+        in_=raw[:, :, lo:hi].rearrange("p j (c i) -> p c j i", i=4),
+    )
+
+
+def tile_picked_place_lin_none_sub_l_kernel(tc, xT, w, gate, offs, out):
+    nc = tc.nc
+    with ExitStack() as ctx:
+        keep = ctx.enter_context(tc.tile_pool(name="keep", bufs=1))
+        psum = ctx.enter_context(tc.psum_pool(name="psum", bufs=1))
+
+        def rows(c, lo, hi):
+            return xT[c * K_PASS : (c + 1) * K_PASS, lo:hi].rearrange("(p j) n -> p j n", j=PACK)
+
+        w_raw = keep.tile([P, PASSES, PACK, N], F32, name="w_raw")
+        nc.sync.dma_start(out=w_raw[:], in_=w.rearrange("(c p j) m -> p c j m", p=P, j=PACK))
+
+        def load(c, lo, hi):
+            raw = keep.tile([P, PACK, hi - lo], F32, name=f"raw_{c}_{lo}")
+            nc.sync.dma_start(out=raw[:], in_=rows(c, lo, hi))
+            return raw
+
+        x0a, x1a, x2a = (load(c, 0, HALF) for c in range(PASSES))
+        offsets = keep.tile([P, S // 16], U16, name="offsets")
+        nc.sync.dma_start(offsets[:], offs)
+        gates = keep.tile([P, S - PIECE], F32, name="gates")
+        nc.sync.dma_start(out=gates[:], in_=gate[:, 0 : S - PIECE])
+        x0b, x1b = (load(c, HALF, S) for c in range(2))
+        x2b = load(2, HALF, HALF + PIECE)
+        x2c = load(2, HALF + PIECE, S)
+        gates_c = keep.tile([P, PIECE], F32, name="gates_c")
+        nc.sync.dma_start(out=gates_c[:], in_=gate[:, S - PIECE : S])
+
+        window = keep.tile([P, T], F32, name="window")
+        nc.vector.memset(window[:], 0.0)
+
+        w_grouped = keep.tile([P, PASSES, N, PACK], BF16, name="w_grouped", align_bytes=64)
+        w_codes = keep.tile([P, PASSES, N], U32, name="w_codes", align_bytes=64)
+        w_scales = keep.tile([P, PASSES, N], U8, name="w_scales", align_bytes=64)
+        for c, copy in enumerate((nc.vector.tensor_copy, nc.vector.tensor_copy, nc.scalar.copy)):
+            interleave(copy, w_grouped[:, c], w_raw[:, c], 0, N)
+        for lo, hi in ((0, 2), (2, 3)):
+            nc.vector.quantize_mx(
+                out=w_codes[:, lo:hi].rearrange("p c m -> p (c m)").bitcast(FP8X4),
+                scales=w_scales[:, lo:hi].rearrange("p c m -> p (c m)"),
+                in_=w_grouped[:, lo:hi].rearrange("p c m j -> p (c m j)"),
+            )
+
+        def quantised(label, raw, lo, width, share):
+            grouped = keep.tile([P, width, PACK], BF16, name="grouped" + label, align_bytes=64)
+            part = raw[:, :, lo : lo + width]
+            if share > 0:
+                interleave(nc.scalar.copy, grouped, part, 0, share)
+            if share < width:
+                interleave(nc.vector.tensor_copy, grouped, part, share, width)
+            codes = keep.tile([P, width], U32, name="codes" + label, align_bytes=64)
+            scales = keep.tile([P, width], U8, name="scales" + label, align_bytes=64)
+            nc.vector.quantize_mx(
+                out=codes[:].bitcast(FP8X4), scales=scales[:], in_=grouped[:].rearrange("p n j -> p (n j)")
+            )
+            return codes, scales
+
+        def multiply(acc, c, operand, lo, width):
+            codes, scales = operand
+            nc.tensor.matmul_mx(
+                out=acc[:],
+                lhsT=w_codes[:, c, :].bitcast(FP8X4),
+                lhsT_scale=w_scales[:, c, :],
+                rhs=codes[:, lo : lo + width].bitcast(FP8X4),
+                rhs_scale=scales[:, lo : lo + width],
+                start=(c == 0),
+                stop=(c == PASSES - 1),
+            )
+
+        def finish(label, acc, gate_cols, first, width):
+            weighted = keep.tile([P, width], F32, name="weighted" + label)
+            nc.vector.tensor_tensor(out=weighted[:], in0=acc[:], in1=gate_cols, op=mybir.AluOpType.mult)
+            for lo in range(0, width, PIECE):
+                cols = slice((first + lo) // 16, (first + lo + PIECE) // 16)
+                nc.vector.tensor_copy(window[:].indirect(offsets[:, cols]), weighted[:, lo : lo + PIECE])
+
+        acc_a = psum.tile([P, HALF], F32, name="acc_a")
+        acc_b = psum.tile([P, PIECE], F32, name="acc_b")
+        acc_c = psum.tile([P, PIECE], F32, name="acc_c")
+
+        q0a = quantised("0a", x0a, 0, HALF, 384)
+        multiply(acc_a, 0, q0a, 0, HALF)
+        q1a = quantised("1a", x1a, 0, HALF, 384)
+        multiply(acc_a, 1, q1a, 0, HALF)
+        q2a = quantised("2a", x2a, 0, HALF, 320)
+        multiply(acc_a, 2, q2a, 0, HALF)
+        finish("a", acc_a, gates[:, 0:HALF], 0, HALF)
+        q0b = quantised("0b", x0b, 0, HALF, HALF)
+        multiply(acc_b, 0, q0b, 0, PIECE)
+        multiply(acc_c, 0, q0b, PIECE, PIECE)
+        q1b = quantised("1b", x1b, 0, HALF, HALF)
+        multiply(acc_b, 1, q1b, 0, PIECE)
+        multiply(acc_c, 1, q1b, PIECE, PIECE)
+        q2b = quantised("2b", x2b, 0, PIECE, PIECE)
+        multiply(acc_b, 2, q2b, 0, PIECE)
+        finish("b", acc_b, gates[:, HALF : HALF + PIECE], HALF, PIECE)
+        q2c = quantised("2c", x2c, 0, PIECE, 96)
+        multiply(acc_c, 2, q2c, 0, PIECE)
+        finish("c", acc_c, gates_c[:], HALF + PIECE, PIECE)
+
+        nc.sync.dma_start(out=out, in_=window[:])

@@ -16,8 +16,10 @@ P = 128
 PACK = 4
 K_PASS = P * PACK
 PASSES = K // K_PASS
-HALF = 512
-PIECE = 256
+CHUNK = 256
+OFFSETS_PER_COLUMN = 16
+
+SCALAR_COLUMNS = (160, CHUNK, CHUNK)
 
 
 def interleave(copy, grouped, raw, lo, hi):
@@ -33,27 +35,27 @@ def tile_picked_place_lin_none_sub_l_kernel(tc, xT, w, gate, offs, out):
         keep = ctx.enter_context(tc.tile_pool(name="keep", bufs=1))
         psum = ctx.enter_context(tc.psum_pool(name="psum", bufs=1))
 
-        def rows(c, lo, hi):
-            return xT[c * K_PASS : (c + 1) * K_PASS, lo:hi].rearrange("(p j) n -> p j n", j=PACK)
-
         w_raw = keep.tile([P, PASSES, PACK, N], F32, name="w_raw")
         nc.sync.dma_start(out=w_raw[:], in_=w.rearrange("(c p j) m -> p c j m", p=P, j=PACK))
 
-        def load(c, lo, hi):
-            raw = keep.tile([P, PACK, hi - lo], F32, name=f"raw_{c}_{lo}")
-            nc.sync.dma_start(out=raw[:], in_=rows(c, lo, hi))
-            return raw
+        x_raw = {}
 
-        x0a, x1a, x2a = (load(c, 0, HALF) for c in range(PASSES))
-        offsets = keep.tile([P, S // 16], U16, name="offsets")
+        def load_chunk(first):
+            for c in range(PASSES):
+                rows = xT[c * K_PASS : (c + 1) * K_PASS, first : first + CHUNK]
+                x_raw[c, first] = keep.tile([P, PACK, CHUNK], F32, name=f"x_raw_{c}_{first}")
+                nc.sync.dma_start(out=x_raw[c, first][:], in_=rows.rearrange("(p j) n -> p j n", j=PACK))
+
+        last = S - CHUNK
+        load_chunk(0)
+        offsets = keep.tile([P, S // OFFSETS_PER_COLUMN], U16, name="offsets")
         nc.sync.dma_start(offsets[:], offs)
-        gates = keep.tile([P, S - PIECE], F32, name="gates")
-        nc.sync.dma_start(out=gates[:], in_=gate[:, 0 : S - PIECE])
-        x0b, x1b = (load(c, HALF, S) for c in range(2))
-        x2b = load(2, HALF, HALF + PIECE)
-        x2c = load(2, HALF + PIECE, S)
-        gates_c = keep.tile([P, PIECE], F32, name="gates_c")
-        nc.sync.dma_start(out=gates_c[:], in_=gate[:, S - PIECE : S])
+        gates = keep.tile([P, last], F32, name="gates")
+        nc.sync.dma_start(out=gates[:], in_=gate[:, 0:last])
+        for first in range(CHUNK, S, CHUNK):
+            load_chunk(first)
+        last_gates = keep.tile([P, CHUNK], F32, name="last_gates")
+        nc.sync.dma_start(out=last_gates[:], in_=gate[:, last:S])
 
         window = keep.tile([P, T], F32, name="window")
         nc.vector.memset(window[:], 0.0)
@@ -62,69 +64,43 @@ def tile_picked_place_lin_none_sub_l_kernel(tc, xT, w, gate, offs, out):
         w_codes = keep.tile([P, PASSES, N], U32, name="w_codes", align_bytes=64)
         w_scales = keep.tile([P, PASSES, N], U8, name="w_scales", align_bytes=64)
         for c, copy in enumerate((nc.vector.tensor_copy, nc.vector.tensor_copy, nc.scalar.copy)):
-            interleave(copy, w_grouped[:, c], w_raw[:, c], 0, N)
-        for lo, hi in ((0, 2), (2, 3)):
+            interleave(copy, w_grouped[:, c, :, :], w_raw[:, c, :, :], 0, N)
+        for lo, hi in ((0, 2), (2, PASSES)):
             nc.vector.quantize_mx(
-                out=w_codes[:, lo:hi].rearrange("p c m -> p (c m)").bitcast(FP8X4),
-                scales=w_scales[:, lo:hi].rearrange("p c m -> p (c m)"),
-                in_=w_grouped[:, lo:hi].rearrange("p c m j -> p (c m j)"),
+                out=w_codes[:, lo:hi, :].rearrange("p c m -> p (c m)").bitcast(FP8X4),
+                scales=w_scales[:, lo:hi, :].rearrange("p c m -> p (c m)"),
+                in_=w_grouped[:, lo:hi, :, :].rearrange("p c m j -> p (c m j)"),
             )
 
-        def quantised(label, raw, lo, width, share):
-            grouped = keep.tile([P, width, PACK], BF16, name="grouped" + label, align_bytes=64)
-            part = raw[:, :, lo : lo + width]
-            if share > 0:
-                interleave(nc.scalar.copy, grouped, part, 0, share)
-            if share < width:
-                interleave(nc.vector.tensor_copy, grouped, part, share, width)
-            codes = keep.tile([P, width], U32, name="codes" + label, align_bytes=64)
-            scales = keep.tile([P, width], U8, name="scales" + label, align_bytes=64)
+        def multiply_pass(acc, c, first):
+            grouped = keep.tile([P, CHUNK, PACK], BF16, name=f"grouped_{c}_{first}", align_bytes=64)
+            border = SCALAR_COLUMNS[c]
+            interleave(nc.scalar.copy, grouped, x_raw[c, first], 0, border)
+            if border < CHUNK:
+                interleave(nc.vector.tensor_copy, grouped, x_raw[c, first], border, CHUNK)
+            codes = keep.tile([P, CHUNK], U32, name=f"codes_{c}_{first}", align_bytes=64)
+            scales = keep.tile([P, CHUNK], U8, name=f"scales_{c}_{first}", align_bytes=64)
             nc.vector.quantize_mx(
                 out=codes[:].bitcast(FP8X4), scales=scales[:], in_=grouped[:].rearrange("p n j -> p (n j)")
             )
-            return codes, scales
-
-        def multiply(acc, c, operand, lo, width):
-            codes, scales = operand
             nc.tensor.matmul_mx(
                 out=acc[:],
                 lhsT=w_codes[:, c, :].bitcast(FP8X4),
                 lhsT_scale=w_scales[:, c, :],
-                rhs=codes[:, lo : lo + width].bitcast(FP8X4),
-                rhs_scale=scales[:, lo : lo + width],
+                rhs=codes[:].bitcast(FP8X4),
+                rhs_scale=scales[:],
                 start=(c == 0),
                 stop=(c == PASSES - 1),
             )
 
-        def finish(label, acc, gate_cols, first, width):
-            weighted = keep.tile([P, width], F32, name="weighted" + label)
-            nc.vector.tensor_tensor(out=weighted[:], in0=acc[:], in1=gate_cols, op=mybir.AluOpType.mult)
-            for lo in range(0, width, PIECE):
-                cols = slice((first + lo) // 16, (first + lo + PIECE) // 16)
-                nc.vector.tensor_copy(window[:].indirect(offsets[:, cols]), weighted[:, lo : lo + PIECE])
-
-        acc_a = psum.tile([P, HALF], F32, name="acc_a")
-        acc_b = psum.tile([P, PIECE], F32, name="acc_b")
-        acc_c = psum.tile([P, PIECE], F32, name="acc_c")
-
-        q0a = quantised("0a", x0a, 0, HALF, 384)
-        multiply(acc_a, 0, q0a, 0, HALF)
-        q1a = quantised("1a", x1a, 0, HALF, 384)
-        multiply(acc_a, 1, q1a, 0, HALF)
-        q2a = quantised("2a", x2a, 0, HALF, 320)
-        multiply(acc_a, 2, q2a, 0, HALF)
-        finish("a", acc_a, gates[:, 0:HALF], 0, HALF)
-        q0b = quantised("0b", x0b, 0, HALF, HALF)
-        multiply(acc_b, 0, q0b, 0, PIECE)
-        multiply(acc_c, 0, q0b, PIECE, PIECE)
-        q1b = quantised("1b", x1b, 0, HALF, HALF)
-        multiply(acc_b, 1, q1b, 0, PIECE)
-        multiply(acc_c, 1, q1b, PIECE, PIECE)
-        q2b = quantised("2b", x2b, 0, PIECE, PIECE)
-        multiply(acc_b, 2, q2b, 0, PIECE)
-        finish("b", acc_b, gates[:, HALF : HALF + PIECE], HALF, PIECE)
-        q2c = quantised("2c", x2c, 0, PIECE, 96)
-        multiply(acc_c, 2, q2c, 0, PIECE)
-        finish("c", acc_c, gates_c[:], HALF + PIECE, PIECE)
+        for first in range(0, S, CHUNK):
+            acc = psum.tile([N, CHUNK], F32, name=f"acc_{first}")
+            for c in range(PASSES):
+                multiply_pass(acc, c, first)
+            weighted = keep.tile([N, CHUNK], F32, name=f"weighted_{first}")
+            chunk_gates = last_gates[:] if first == last else gates[:, first : first + CHUNK]
+            nc.vector.tensor_tensor(out=weighted[:], in0=acc[:], in1=chunk_gates, op=mybir.AluOpType.mult)
+            entries = offsets[:, first // OFFSETS_PER_COLUMN : (first + CHUNK) // OFFSETS_PER_COLUMN]
+            nc.vector.tensor_copy(window[:].indirect(entries), weighted[:])
 
         nc.sync.dma_start(out=out, in_=window[:])

from contextlib import ExitStack

import concourse.mybir as mybir

K, S, N, T = 1536, 1024, 128, 2048
FLOPS = 2 * K * S * N

F32 = mybir.dt.float32
BF16 = mybir.dt.bfloat16
U32 = mybir.dt.uint32
U16 = mybir.dt.uint16
U8 = mybir.dt.uint8
FP8X4 = mybir.dt.float8_e4m3fn_x4

P = 128
PACK = 4
K_PASS = P * PACK
PASSES = K // K_PASS
CHUNK = 256
OFFSETS_PER_COLUMN = 16

SCALAR_COLUMNS = (160, CHUNK, CHUNK)


def interleave(copy, grouped, raw, lo, hi):
    copy(
        out=grouped[:, lo:hi, :].rearrange("p (c i) j -> p c j i", i=4),
        in_=raw[:, :, lo:hi].rearrange("p j (c i) -> p c j i", i=4),
    )


def tile_picked_place_lin_none_sub_l_kernel(tc, xT, w, gate, offs, out):
    nc = tc.nc
    with ExitStack() as ctx:
        keep = ctx.enter_context(tc.tile_pool(name="keep", bufs=1))
        psum = ctx.enter_context(tc.psum_pool(name="psum", bufs=1))

        w_raw = keep.tile([P, PASSES, PACK, N], F32, name="w_raw")
        nc.sync.dma_start(out=w_raw[:], in_=w.rearrange("(c p j) m -> p c j m", p=P, j=PACK))

        x_raw = {}

        def load_chunk(first):
            for c in range(PASSES):
                rows = xT[c * K_PASS : (c + 1) * K_PASS, first : first + CHUNK]
                x_raw[c, first] = keep.tile([P, PACK, CHUNK], F32, name=f"x_raw_{c}_{first}")
                nc.sync.dma_start(out=x_raw[c, first][:], in_=rows.rearrange("(p j) n -> p j n", j=PACK))

        last = S - CHUNK
        load_chunk(0)
        offsets = keep.tile([P, S // OFFSETS_PER_COLUMN], U16, name="offsets")
        nc.sync.dma_start(offsets[:], offs)
        gates = keep.tile([P, last], F32, name="gates")
        nc.sync.dma_start(out=gates[:], in_=gate[:, 0:last])
        for first in range(CHUNK, S, CHUNK):
            load_chunk(first)
        last_gates = keep.tile([P, CHUNK], F32, name="last_gates")
        nc.sync.dma_start(out=last_gates[:], in_=gate[:, last:S])

        window = keep.tile([P, T], F32, name="window")
        nc.vector.memset(window[:], 0.0)

        w_grouped = keep.tile([P, PASSES, N, PACK], BF16, name="w_grouped", align_bytes=64)
        w_codes = keep.tile([P, PASSES, N], U32, name="w_codes", align_bytes=64)
        w_scales = keep.tile([P, PASSES, N], U8, name="w_scales", align_bytes=64)
        for c, copy in enumerate((nc.vector.tensor_copy, nc.vector.tensor_copy, nc.scalar.copy)):
            interleave(copy, w_grouped[:, c, :, :], w_raw[:, c, :, :], 0, N)
        for lo, hi in ((0, 2), (2, PASSES)):
            nc.vector.quantize_mx(
                out=w_codes[:, lo:hi, :].rearrange("p c m -> p (c m)").bitcast(FP8X4),
                scales=w_scales[:, lo:hi, :].rearrange("p c m -> p (c m)"),
                in_=w_grouped[:, lo:hi, :, :].rearrange("p c m j -> p (c m j)"),
            )

        def multiply_pass(acc, c, first):
            grouped = keep.tile([P, CHUNK, PACK], BF16, name=f"grouped_{c}_{first}", align_bytes=64)
            border = SCALAR_COLUMNS[c]
            interleave(nc.scalar.copy, grouped, x_raw[c, first], 0, border)
            if border < CHUNK:
                interleave(nc.vector.tensor_copy, grouped, x_raw[c, first], border, CHUNK)
            codes = keep.tile([P, CHUNK], U32, name=f"codes_{c}_{first}", align_bytes=64)
            scales = keep.tile([P, CHUNK], U8, name=f"scales_{c}_{first}", align_bytes=64)
            nc.vector.quantize_mx(
                out=codes[:].bitcast(FP8X4), scales=scales[:], in_=grouped[:].rearrange("p n j -> p (n j)")
            )
            nc.tensor.matmul_mx(
                out=acc[:],
                lhsT=w_codes[:, c, :].bitcast(FP8X4),
                lhsT_scale=w_scales[:, c, :],
                rhs=codes[:].bitcast(FP8X4),
                rhs_scale=scales[:],
                start=(c == 0),
                stop=(c == PASSES - 1),
            )

        for first in range(0, S, CHUNK):
            acc = psum.tile([N, CHUNK], F32, name=f"acc_{first}")
            for c in range(PASSES):
                multiply_pass(acc, c, first)
            weighted = keep.tile([N, CHUNK], F32, name=f"weighted_{first}")
            chunk_gates = last_gates[:] if first == last else gates[:, first : first + CHUNK]
            nc.vector.tensor_tensor(out=weighted[:], in0=acc[:], in1=chunk_gates, op=mybir.AluOpType.mult)
            entries = offsets[:, first // OFFSETS_PER_COLUMN : (first + CHUNK) // OFFSETS_PER_COLUMN]
            nc.vector.tensor_copy(window[:].indirect(entries), weighted[:])

        nc.sync.dma_start(out=out, in_=window[:])
